import numpy as np
import ml_dtypes


def mxq(x, axis, fmt="e4m3"):
    dtype, down = {"e4m3": (ml_dtypes.float8_e4m3fn, 7), "e5m2": (ml_dtypes.float8_e5m2, 14)}[fmt]
    v = np.moveaxis(np.asarray(x, np.float32).astype(ml_dtypes.bfloat16).astype(np.float64), axis, -1)
    blocks = v.reshape(v.shape[:-1] + (-1, 32))
    amax = np.abs(blocks).max(-1, keepdims=True)
    byte = np.maximum(np.where(amax > 0, np.frexp(amax)[1] - 1 + 127, 0) - down, 1)
    scale = np.exp2(byte - 127.0)
    codes = (blocks / scale).astype(np.float32).astype(dtype).astype(np.float64)
    return np.moveaxis((codes * scale).reshape(v.shape), -1, axis)


WIDE = False


def mx_kscale(k):
    if not WIDE:
        return np.ones(k)
    levels = np.array([30, -30])
    if k % 512:
        return np.exp2(np.random.permutation(np.resize(levels, k // 32))).repeat(32)
    a = np.empty((k // 512, 16))
    for p in range(k // 512):
        a[p, :8] = np.random.permutation(np.resize(levels, 8))
        for g in range(8):
            far = levels[np.abs(levels - a[p, g]) >= 10]
            a[p, g + 8] = far[np.random.randint(len(far))]
    return np.exp2(a.ravel()).repeat(32)


def f64(x):
    return np.asarray(x).astype(np.float64)


def striped(idx):
    return np.tile(np.asarray(idx).reshape(-1, 16).T, (8, 1)).astype(np.uint16)


def unstriped(offs):
    return offs[:16].T.reshape(-1).astype(np.int64)


E2M1 = np.array([0.0, 0.5, 1.0, 1.5, 2.0, 3.0, 4.0, 6.0, -0.0, -0.5, -1.0, -1.5, -2.0, -3.0, -4.0, -6.0])


def pack_weight(w, fmt):
    k, n = w.shape
    w = f64(np.asarray(w, np.float32).astype(ml_dtypes.bfloat16)).reshape(k // 32, 32, n)
    amax = np.abs(w).max(1)
    if fmt in ("e4m3", "e5m2"):
        byte = np.frexp(amax)[1] - 1 + 127 - (7 if fmt == "e4m3" else 14)
    else:
        mant, ex = np.frexp(amax / 6.0)
        byte = np.where(mant > 0.5, ex, ex - 1) + 127
    byte = np.clip(np.where(amax > 0, byte, 1), 1, 254)
    scaled = (w * np.exp2(127.0 - byte)[:, None, :]).reshape(k, n).astype(np.float32)
    by_word = np.ascontiguousarray(scaled.reshape(k // 512, 128, 4, n).transpose(0, 1, 3, 2))
    if fmt in ("e4m3", "e5m2"):
        words = by_word.astype(ml_dtypes.float8_e4m3fn if fmt == "e4m3" else ml_dtypes.float8_e5m2).view(np.uint8)
    else:
        c = by_word.astype(ml_dtypes.float4_e2m1fn).view(np.uint8) & 0xF
        words = (c[..., 0::2] | (c[..., 1::2] << 4)).reshape(k // 512, 128, 2 * n)
    return np.ascontiguousarray(words), np.ascontiguousarray(byte.astype(np.uint8).reshape(k // 512, 16, n))


def unpack_weight(words, scales, fmt):
    g, _, n = scales.shape
    words = np.ascontiguousarray(words).reshape(g, 128, n, -1)
    if fmt in ("e4m3", "e5m2"):
        vals = words.view(ml_dtypes.float8_e4m3fn if fmt == "e4m3" else ml_dtypes.float8_e5m2).astype(np.float64)
    else:
        nib = np.empty((g, 128, n, 4), np.uint8)
        nib[..., 0::2] = words & 0xF
        nib[..., 1::2] = words >> 4
        vals = E2M1[nib]
    vals = vals * np.repeat(np.exp2(scales.astype(np.float64) - 127.0), 8, axis=1)[..., None]
    return vals.transpose(0, 1, 3, 2).reshape(g * 512, n)


K, T, J, R, F, N, Z = 512, 512, 256, 512, 512, 256, 512


def setup_inputs():
    n = np.random.standard_normal
    idx = np.random.permutation(T)[:J]
    idx2 = np.random.permutation(Z)[:J]
    fk = mx_kscale(K)
    fr = mx_kscale(R)
    ff = mx_kscale(F)
    wp = pack_weight(n((K, R)) * 1 / np.sqrt(K) * fk[:, None] * fr, "e2m1")
    sxp = pack_weight(n((F, J)) / ff[:, None], "e5m2")
    w2p = pack_weight(n((F, R)) * 1 / np.sqrt(F) * ff[:, None] * fr, "e2m1")
    wbp = pack_weight(n((R, N)) * 1 / np.sqrt(R) / fr[:, None], "e2m1")
    return {
        "xf": (n((K, T))).astype(np.float32),
        "ow": (n((K, J)) * 0.7).astype(np.float32),
        "fk": (np.random.uniform(0.5, 2.0, (K, 1)) / fk[:, None]).astype(np.float32),
        "w_words": wp[0],
        "w_scales": wp[1],
        "sx_words": sxp[0],
        "sx_scales": sxp[1],
        "w2_words": w2p[0],
        "w2_scales": w2p[1],
        "wb_words": wbp[0],
        "wb_scales": wbp[1],
        "tz": (n((N, Z))).astype(np.float32),
        "offs": striped(idx),
        "offs2": striped(idx2),
    }


def reference(xf, ow, fk, w_words, w_scales, sx_words, sx_scales, w2_words, w2_scales, wb_words, wb_scales, tz, offs, offs2):
    idx = unstriped(offs)
    idx2 = unstriped(offs2)
    wu = unpack_weight(w_words, w_scales, "e2m1")
    sxu = unpack_weight(sx_words, sx_scales, "e5m2")
    w2u = unpack_weight(w2_words, w2_scales, "e2m1")
    wbu = unpack_weight(wb_words, wb_scales, "e2m1")
    u = (f64(xf)[:, idx] - f64(ow)) * f64(fk)
    uq = mxq(u, 0, "e4m3")
    a = wu.T @ uq
    q = w2u.T @ sxu
    y1 = np.pad(q, ((0, 0), (1, 0)))[:, :J]
    hid = np.maximum(a, q - 0.6 * y1)
    hidq = mxq(hid, 0, "e5m2")
    p = wbu.T @ hidq
    y = p * f64(tz)[:, idx2]
    return y

@@ -1,0 +1,195 @@
+from contextlib import ExitStack
+
+import concourse.mybir as mybir
+
+K, T, J, R, F, N, Z = 512, 512, 256, 512, 512, 256, 512
+FLOPS = 2 * K * R * J + 2 * F * R * J + 2 * R * N * J
+
+F32 = mybir.dt.float32
+BF16 = mybir.dt.bfloat16
+I32 = mybir.dt.int32
+U32 = mybir.dt.uint32
+U16 = mybir.dt.uint16
+U8 = mybir.dt.uint8
+E4M3X4 = mybir.dt.float8_e4m3fn_x4
+E5M2X4 = mybir.dt.float8_e5m2_x4
+E2M1X4 = mybir.dt.float4_e2m1fn_x4
+ALU = mybir.AluOpType
+COPY = mybir.ActivationFunctionType.Copy
+
+P = 128
+PACK = 4
+HALF = 128
+PAD = 4
+
+
+def tile_list_two_offsetpicks_own_stepgap_timeslook_kernel(
+    tc, xf, ow, fk, w_words, w_scales, sx_words, sx_scales, w2_words, w2_scales, wb_words, wb_scales, tz, offs, offs2, out
+):
+    nc = tc.nc
+    with ExitStack() as ctx:
+        lists = ctx.enter_context(tc.tile_pool(name="lists", bufs=1))
+        sb = ctx.enter_context(tc.tile_pool(name="sb", bufs=1))
+        ps = ctx.enter_context(tc.psum_pool(name="ps", bufs=1))
+
+        idx = lists.tile([P, J // 16], U16, name="idx")
+        idx2 = lists.tile([P, J // 16], U16, name="idx2")
+
+        def plane(name, width):
+            return sb.tile([P, width], U8, name=name, align_bytes=64)
+
+        def load_scales_filled(queue, t, scales):
+            for quad in range(4):
+                rows = scales[0, 4 * quad : 4 * quad + 4, :].bitcast(I32)
+                queue.dma_start(
+                    out=t[32 * quad : 32 * quad + 32, :].bitcast(I32),
+                    in_=rows.unsqueeze(0).to_broadcast([8, 4, rows.shape[1]]),
+                )
+
+        def load_scales(queue, t, scales):
+            for quad in range(4):
+                queue.dma_start(
+                    out=t[32 * quad : 32 * quad + 4, :].bitcast(I32),
+                    in_=scales[0, 4 * quad : 4 * quad + 4, :].bitcast(I32),
+                )
+
+        w2s_raw = plane("w2s_raw", R)
+        sxs = plane("sxs", J)
+        ws_raw = plane("ws_raw", R)
+        wbs = plane("wbs", N)
+        qs = sb.tile([P, PACK, PAD + J], F32, name="qs")
+        nc.gpsimd.memset(qs[:, :, 0:PAD], 0.0)
+
+        w2w_raw = sb.tile([P, 2 * R], U8, name="w2w_raw", align_bytes=64)
+        ww_raw = sb.tile([P, 2 * R], U8, name="ww_raw", align_bytes=64)
+        sxw = sb.tile([P, J], U32, name="sxw", align_bytes=64)
+        wbw = sb.tile([P, 2 * N], U8, name="wbw", align_bytes=64)
+        x01 = sb.tile([P, 2, T], F32, name="x01")
+        x2 = sb.tile([P, T], F32, name="x2")
+        x3 = sb.tile([P, T], F32, name="x3")
+        ow_sb = sb.tile([P, PACK, J], F32, name="ow_sb")
+        fk_sb = sb.tile([P, PACK], F32, name="fk_sb")
+        tz_sb = sb.tile([P, 2, Z], F32, name="tz_sb")
+
+        xv = xf.rearrange("(p t) c -> p t c", t=PACK)
+        load_scales_filled(nc.scalar, w2s_raw, w2_scales)
+        nc.sync.dma_start(out=w2w_raw[:].bitcast(I32), in_=w2_words[0].bitcast(I32))
+        nc.sync.dma_start(out=sxw[:].bitcast(I32), in_=sx_words[0].rearrange("p n t -> p (n t)").bitcast(I32))
+        nc.sync.dma_start(idx[:], offs)
+        nc.sync.dma_start(out=x01[:], in_=xv[:, 0:2, :])
+        load_scales(nc.sync, sxs, sx_scales)
+        nc.sync.dma_start(out=ow_sb[:], in_=ow.rearrange("(p t) c -> p t c", t=PACK))
+        nc.sync.dma_start(out=ww_raw[:].bitcast(I32), in_=w_words[0].bitcast(I32))
+        nc.sync.dma_start(out=x2[:], in_=xv[:, 2, :])
+        nc.sync.dma_start(out=x3[:], in_=xv[:, 3, :])
+        load_scales_filled(nc.sync, ws_raw, w_scales)
+        nc.sync.dma_start(out=fk_sb[:], in_=fk.rearrange("(p t) o -> p (t o)", t=PACK))
+        nc.sync.dma_start(idx2[:], offs2)
+        nc.sync.dma_start(out=tz_sb[:], in_=tz.rearrange("(h p) z -> p h z", p=P))
+        nc.sync.dma_start(out=wbw[:].bitcast(I32), in_=wb_words[0].bitcast(I32))
+        load_scales(nc.sync, wbs, wb_scales)
+
+        def deal(name, raw, dtype, run):
+            t = sb.tile([P, raw.shape[1]], U8, name=name, align_bytes=64)
+            nc.vector.tensor_copy(
+                out=t[:].bitcast(dtype).rearrange("p (t c i) -> p c t i", t=PACK, i=run),
+                in_=raw[:].bitcast(dtype).rearrange("p (c i t) -> p c t i", t=PACK, i=run),
+            )
+            return t
+
+        def first_stage(name, words, scales, rhs, rhs_scale):
+            bank = ps.tile([P, PACK, HALF], F32, name=name)
+            for t in range(PACK):
+                nc.tensor.matmul_mx(
+                    out=bank[:, t, :],
+                    lhsT=words[:, 2 * P * t : 2 * P * (t + 1)].bitcast(E2M1X4),
+                    lhsT_scale=scales[:, P * t : P * (t + 1)],
+                    rhs=rhs,
+                    rhs_scale=rhs_scale,
+                    start=True,
+                    stop=True,
+                )
+            return bank
+
+        halves = [slice(HALF * h, HALF * (h + 1)) for h in range(2)]
+
+        w2w = deal("w2w", w2w_raw, U16, 8)
+        w2s = deal("w2s", w2s_raw, U8, 16)
+        step = sb.tile([P, PACK, J], F32, name="step")
+        q_banks = []
+        for h, cols in enumerate(halves):
+            q = first_stage("q%d" % h, w2w, w2s, sxw[:, cols].bitcast(E5M2X4), sxs[:, cols])
+            nc.scalar.copy(out=qs[:, :, PAD + HALF * h : PAD + HALF * (h + 1)], in_=q[:])
+            q_banks.append(q)
+
+        picked = sb.tile([P, PACK, J], F32, name="picked")
+        diff = sb.tile([P, PACK, J], F32, name="diff")
+        windows = [x01[:, 0, :], x01[:, 1, :], x2[:], x3[:]]
+        for t in range(PACK):
+            nc.scalar.activation(picked[:, t, :], windows[t].indirect(idx[:]), COPY)
+        ww = deal("ww", ww_raw, U16, 8)
+        for t in range(2):
+            nc.vector.tensor_tensor(out=diff[:, t, :], in0=picked[:, t, :], in1=ow_sb[:, t, :], op=ALU.subtract)
+        for h, cols in enumerate(halves):
+            nc.vector.scalar_tensor_tensor(
+                out=step[:, :, cols],
+                in0=qs[:, :, PAD - 1 + HALF * h : PAD - 1 + HALF * (h + 1)],
+                scalar=-0.6,
+                in1=q_banks[h][:],
+                op0=ALU.mult,
+                op1=ALU.add,
+            )
+        ws = deal("ws", ws_raw, U8, 16)
+        for t in range(2, PACK):
+            nc.vector.tensor_tensor(out=diff[:, t, :], in0=picked[:, t, :], in1=ow_sb[:, t, :], op=ALU.subtract)
+
+        tz_picked = sb.tile([P, 2, J], F32, name="tz_picked")
+        for b in range(2):
+            nc.scalar.activation(tz_picked[:, b, :], tz_sb[:, b, :].indirect(idx2[:]), COPY)
+
+        def pairs(ap):
+            return ap.rearrange("p t (c i) -> p c t i", i=2)
+
+        def woven(t):
+            return t[:].rearrange("p (c i t) -> p c t i", t=PACK, i=2)
+
+        def quantise(name, src, dtype):
+            codes = sb.tile([P, HALF], U32, name=name + "_codes", align_bytes=64)
+            scales = sb.tile([P, HALF], U8, name=name + "_scales", align_bytes=64)
+            nc.vector.quantize_mx(out=codes[:].bitcast(dtype), scales=scales[:], in_=src[:])
+            return codes[:].bitcast(dtype), scales[:]
+
+        fk_wide = fk_sb[:].unsqueeze(1).unsqueeze(3).to_broadcast([P, HALF // 2, PACK, 2])
+        u = [sb.tile([P, PACK * HALF], BF16, name="u%d" % h, align_bytes=64) for h in range(2)]
+        for h, cols in enumerate(halves):
+            nc.vector.tensor_tensor(out=woven(u[h]), in0=pairs(diff[:, :, cols]), in1=fk_wide, op=ALU.mult)
+        a_banks = []
+        for h in range(2):
+            codes, scales = quantise("u%d" % h, u[h], E4M3X4)
+            a_banks.append(first_stage("a%d" % h, ww, ws, codes, scales))
+
+        hid = [sb.tile([P, PACK * HALF], BF16, name="hid%d" % h, align_bytes=64) for h in range(2)]
+        for h, cols in enumerate(halves):
+            nc.vector.tensor_tensor(out=woven(hid[h]), in0=pairs(a_banks[h][:]), in1=pairs(step[:, :, cols]), op=ALU.max)
+        p_banks = []
+        for h in range(2):
+            codes, scales = quantise("hid%d" % h, hid[h], E5M2X4)
+            bank = ps.tile([P, 2, HALF], F32, name="p%d" % h)
+            for b in range(2):
+                nc.tensor.matmul_mx(
+                    out=bank[:, b, :],
+                    lhsT=wbw[:, 2 * P * b : 2 * P * (b + 1)].bitcast(E2M1X4),
+                    lhsT_scale=wbs[:, P * b : P * (b + 1)],
+                    rhs=codes,
+                    rhs_scale=scales,
+                    start=True,
+                    stop=True,
+                )
+            p_banks.append(bank)
+
+        ov = out.rearrange("(b p) j -> p b j", p=P)
+        for h, cols in enumerate(halves):
+            y = sb.tile([P, 2, HALF], F32, name="y%d" % h)
+            nc.vector.tensor_tensor(out=y[:], in0=p_banks[h][:], in1=tz_picked[:, :, cols], op=ALU.mult)
+            queue = nc.sync if h == 0 else nc.scalar
+            queue.dma_start(out=ov[:, :, cols], in_=y[:])

@@ -30,70 +30,72 @@ def tile_list_two_offsetpicks_own_stepgap_timeslook_kernel(
     with ExitStack() as ctx:
         lists = ctx.enter_context(tc.tile_pool(name="lists", bufs=1))
         sb = ctx.enter_context(tc.tile_pool(name="sb", bufs=1))
+        shared = ctx.enter_context(tc.tile_pool(name="shared", bufs=1))
         ps = ctx.enter_context(tc.psum_pool(name="ps", bufs=1))
 
         idx = lists.tile([P, J // 16], U16, name="idx")
         idx2 = lists.tile([P, J // 16], U16, name="idx2")
 
-        def plane(name, width):
-            return sb.tile([P, width], U8, name=name, align_bytes=64)
-
-        def load_scales_filled(queue, t, scales):
-            for quad in range(4):
-                rows = scales[0, 4 * quad : 4 * quad + 4, :].bitcast(I32)
-                queue.dma_start(
-                    out=t[32 * quad : 32 * quad + 32, :].bitcast(I32),
-                    in_=rows.unsqueeze(0).to_broadcast([8, 4, rows.shape[1]]),
-                )
-
-        def load_scales(queue, t, scales):
-            for quad in range(4):
-                queue.dma_start(
-                    out=t[32 * quad : 32 * quad + 4, :].bitcast(I32),
-                    in_=scales[0, 4 * quad : 4 * quad + 4, :].bitcast(I32),
-                )
-
-        w2s_raw = plane("w2s_raw", R)
-        sxs = plane("sxs", J)
-        ws_raw = plane("ws_raw", R)
-        wbs = plane("wbs", N)
         qs = sb.tile([P, PACK, PAD + J], F32, name="qs")
         nc.gpsimd.memset(qs[:, :, 0:PAD], 0.0)
 
-        w2w_raw = sb.tile([P, 2 * R], U8, name="w2w_raw", align_bytes=64)
-        ww_raw = sb.tile([P, 2 * R], U8, name="ww_raw", align_bytes=64)
+        staged = shared.tile([P, 2 * R], U8, name="staged", offset=3 * R)
+        planes = sb.tile([P, 2 * R + J], U8, name="planes", align_bytes=64)
+        w2s = planes[:, 0:R]
+        ws = planes[:, R : 2 * R]
+        sxs = planes[:, 2 * R : 2 * R + J]
+        wbs = sb.tile([P, N], U8, name="wbs", align_bytes=64)
+        w2w_raw = sb.tile([P, 2 * R], U8, name="w2w_raw", tag="late_words", align_bytes=64)
         sxw = sb.tile([P, J], U32, name="sxw", align_bytes=64)
-        wbw = sb.tile([P, 2 * N], U8, name="wbw", align_bytes=64)
-        x01 = sb.tile([P, 2, T], F32, name="x01")
-        x2 = sb.tile([P, T], F32, name="x2")
-        x3 = sb.tile([P, T], F32, name="x3")
-        ow_sb = sb.tile([P, PACK, J], F32, name="ow_sb")
+        x01 = sb.tile([P, 2, T], F32, name="x01", tag="table")
+        x23 = sb.tile([P, 2, T], F32, name="x23")
+        ow01 = sb.tile([P, 2, J], F32, name="ow01")
+        ow23 = sb.tile([P, 2, J], F32, name="ow23")
         fk_sb = sb.tile([P, PACK], F32, name="fk_sb")
-        tz_sb = sb.tile([P, 2, Z], F32, name="tz_sb")
+
+        warm_in = sb.tile([P, 8], F32, name="warm_in")
+        warm_out = sb.tile([P, 8], F32, name="warm_out")
+        nc.gpsimd.memset(warm_in[:], 0.0)
+        nc.scalar.activation(warm_out[:], warm_in[:], COPY)
 
         xv = xf.rearrange("(p t) c -> p t c", t=PACK)
-        load_scales_filled(nc.scalar, w2s_raw, w2_scales)
+        owv = ow.rearrange("(p t) c -> p t c", t=PACK)
+        nc.gpsimd.dma_start(out=fk_sb[:], in_=fk.rearrange("(p t) o -> p (t o)", t=PACK))
+        for quad in range(4):
+            nc.gpsimd.dma_start(
+                out=wbs[32 * quad : 32 * quad + 4, :].bitcast(I32),
+                in_=wb_scales[0, 4 * quad : 4 * quad + 4, :].bitcast(I32),
+            )
+        for c, scales in enumerate((w2_scales, w_scales)):
+            rows = scales[0].bitcast(I32)
+            nc.sync.dma_start(
+                out=staged[:, R * c : R * (c + 1)].bitcast(I32),
+                in_=rows.unsqueeze(1).to_broadcast([16, P // 16, R // 4]),
+            )
+        nc.sync.dma_start(out=sxs[0:P:8, :].bitcast(I32), in_=sx_scales[0].bitcast(I32))
+        nc.sync.dma_start(out=x01[:], in_=xv[:, 0:2, :])
+        nc.sync.dma_start(idx[:], offs)
+        nc.sync.dma_start(idx2[:], offs2)
+        nc.sync.dma_start(out=ow01[:], in_=owv[:, 0:2, :])
+        nc.sync.dma_start(out=x23[:], in_=xv[:, 2:4, :])
+        nc.sync.dma_start(out=ow23[:], in_=owv[:, 2:4, :])
         nc.sync.dma_start(out=w2w_raw[:].bitcast(I32), in_=w2_words[0].bitcast(I32))
         nc.sync.dma_start(out=sxw[:].bitcast(I32), in_=sx_words[0].rearrange("p n t -> p (n t)").bitcast(I32))
-        nc.sync.dma_start(idx[:], offs)
-        nc.sync.dma_start(out=x01[:], in_=xv[:, 0:2, :])
-        load_scales(nc.sync, sxs, sx_scales)
-        nc.sync.dma_start(out=ow_sb[:], in_=ow.rearrange("(p t) c -> p t c", t=PACK))
-        nc.sync.dma_start(out=ww_raw[:].bitcast(I32), in_=w_words[0].bitcast(I32))
-        nc.sync.dma_start(out=x2[:], in_=xv[:, 2, :])
-        nc.sync.dma_start(out=x3[:], in_=xv[:, 3, :])
-        load_scales_filled(nc.sync, ws_raw, w_scales)
-        nc.sync.dma_start(out=fk_sb[:], in_=fk.rearrange("(p t) o -> p (t o)", t=PACK))
-        nc.sync.dma_start(idx2[:], offs2)
-        nc.sync.dma_start(out=tz_sb[:], in_=tz.rearrange("(h p) z -> p h z", p=P))
-        nc.sync.dma_start(out=wbw[:].bitcast(I32), in_=wb_words[0].bitcast(I32))
-        load_scales(nc.sync, wbs, wb_scales)
 
-        def deal(name, raw, dtype, run):
-            t = sb.tile([P, raw.shape[1]], U8, name=name, align_bytes=64)
+        nc.vector.tensor_copy(
+            out=planes[:, 0 : 2 * R].rearrange("p (w t c i) -> p w c t i", w=2, t=PACK, i=16),
+            in_=staged[:].rearrange("p (w c i t) -> p w c t i", w=2, t=PACK, i=16),
+        )
+        for r in range(1, 4):
+            nc.sync.dma_start(out=planes[r:P:32, :].bitcast(I32), in_=planes[8 * r : P : 32, :].bitcast(I32))
+        ww_raw = shared.tile([P, 2 * R], U8, name="ww_raw", offset=4 * R)
+        nc.sync.dma_start(out=ww_raw[:].bitcast(I32), in_=w_words[0].bitcast(I32))
+
+        def deal(name, raw):
+            t = sb.tile([P, 2 * R], U8, name=name, align_bytes=64)
             nc.vector.tensor_copy(
-                out=t[:].bitcast(dtype).rearrange("p (t c i) -> p c t i", t=PACK, i=run),
-                in_=raw[:].bitcast(dtype).rearrange("p (c i t) -> p c t i", t=PACK, i=run),
+                out=t[:].bitcast(U16).rearrange("p (t c i) -> p c t i", t=PACK, i=8),
+                in_=raw[:].bitcast(U16).rearrange("p (c i t) -> p c t i", t=PACK, i=8),
             )
             return t
 
@@ -112,40 +114,38 @@ def tile_list_two_offsetpicks_own_stepgap_timeslook_kernel(
             return bank
 
         halves = [slice(HALF * h, HALF * (h + 1)) for h in range(2)]
+        list_halves = [idx[:, 0 : HALF // 16], idx[:, HALF // 16 :]]
 
-        w2w = deal("w2w", w2w_raw, U16, 8)
-        w2s = deal("w2s", w2s_raw, U8, 16)
-        step = sb.tile([P, PACK, J], F32, name="step")
-        q_banks = []
-        for h, cols in enumerate(halves):
-            q = first_stage("q%d" % h, w2w, w2s, sxw[:, cols].bitcast(E5M2X4), sxs[:, cols])
-            nc.scalar.copy(out=qs[:, :, PAD + HALF * h : PAD + HALF * (h + 1)], in_=q[:])
-            q_banks.append(q)
-
-        picked = sb.tile([P, PACK, J], F32, name="picked")
-        diff = sb.tile([P, PACK, J], F32, name="diff")
-        windows = [x01[:, 0, :], x01[:, 1, :], x2[:], x3[:]]
-        for t in range(PACK):
-            nc.scalar.activation(picked[:, t, :], windows[t].indirect(idx[:]), COPY)
-        ww = deal("ww", ww_raw, U16, 8)
-        for t in range(2):
-            nc.vector.tensor_tensor(out=diff[:, t, :], in0=picked[:, t, :], in1=ow_sb[:, t, :], op=ALU.subtract)
-        for h, cols in enumerate(halves):
-            nc.vector.scalar_tensor_tensor(
-                out=step[:, :, cols],
-                in0=qs[:, :, PAD - 1 + HALF * h : PAD - 1 + HALF * (h + 1)],
-                scalar=-0.6,
-                in1=q_banks[h][:],
-                op0=ALU.mult,
-                op1=ALU.add,
+        def scaled_pairs(dst, diff, factors):
+            nc.vector.tensor_tensor(
+                out=dst.rearrange("p (c i t) -> p c t i", t=2, i=4),
+                in0=diff.rearrange("p t (c i) -> p c t i", i=4),
+                in1=factors.unsqueeze(1).unsqueeze(3).to_broadcast([P, HALF // 4, 2, 4]),
+                op=ALU.mult,
             )
-        ws = deal("ws", ws_raw, U8, 16)
-        for t in range(2, PACK):
-            nc.vector.tensor_tensor(out=diff[:, t, :], in0=picked[:, t, :], in1=ow_sb[:, t, :], op=ALU.subtract)
 
-        tz_picked = sb.tile([P, 2, J], F32, name="tz_picked")
-        for b in range(2):
-            nc.scalar.activation(tz_picked[:, b, :], tz_sb[:, b, :].indirect(idx2[:]), COPY)
+        paired = [sb.tile([P, 2, 2 * HALF], BF16, name="paired%d" % h) for h in range(2)]
+        picked01 = shared.tile([P, 2, J], F32, name="picked01", offset=0)
+        diff01 = sb.tile([P, 2, J], F32, name="diff01")
+        nc.scalar.activation(picked01[:, 0, :], x01[:, 0, :].indirect(idx[:]), COPY)
+        nc.vector.tensor_copy(picked01[:, 1, :], x01[:, 1, :].indirect(idx[:]))
+        for cols in halves:
+            nc.vector.tensor_tensor(out=diff01[:, :, cols], in0=picked01[:, :, cols], in1=ow01[:, :, cols], op=ALU.subtract)
+        tz_sb = sb.tile([P, 2, Z], F32, name="tz_sb", tag="table")
+        nc.sync.dma_start(out=tz_sb[:], in_=tz.rearrange("(h p) z -> p h z", p=P))
+        for h, cols in enumerate(halves):
+            scaled_pairs(paired[h][:, 0, :], diff01[:, :, cols], fk_sb[:, 0:2])
+
+        picked23 = sb.tile([P, 2, J], F32, name="picked23")
+        diff23 = sb.tile([P, 2, J], F32, name="diff23")
+        for h, cols in enumerate(halves):
+            for t in range(2):
+                nc.scalar.activation(picked23[:, t, cols], x23[:, t, :].indirect(list_halves[h]), COPY)
+
+        def scaled_pairs_late(h):
+            dst = paired[h][:, 1, :].rearrange("p (j t) -> p t j", t=2)
+            for t in range(2):
+                nc.scalar.activation(dst[:, t, :], diff23[:, t, halves[h]], COPY, scale=fk_sb[:, 2 + t : 3 + t])
 
         def pairs(ap):
             return ap.rearrange("p t (c i) -> p c t i", i=2)
@@ -159,14 +159,51 @@ def tile_list_two_offsetpicks_own_stepgap_timeslook_kernel(
             nc.vector.quantize_mx(out=codes[:].bitcast(dtype), scales=scales[:], in_=src[:])
             return codes[:].bitcast(dtype), scales[:]
 
-        fk_wide = fk_sb[:].unsqueeze(1).unsqueeze(3).to_broadcast([P, HALF // 2, PACK, 2])
+        def subtract23(h):
+            cols = halves[h]
+            nc.vector.tensor_tensor(out=diff23[:, :, cols], in0=picked23[:, :, cols], in1=ow23[:, :, cols], op=ALU.subtract)
+
         u = [sb.tile([P, PACK * HALF], BF16, name="u%d" % h, align_bytes=64) for h in range(2)]
+
+        def weave(h):
+            nc.vector.tensor_copy(
+                out=u[h][:].bitcast(I32).rearrange("p (c i u) -> p c u i", u=2, i=2),
+                in_=paired[h][:].bitcast(I32).rearrange("p u (c i) -> p c u i", i=2),
+            )
+
+        subtract23(0)
+        scaled_pairs_late(0)
+        w2w = deal("w2w", w2w_raw)
+        wbw = sb.tile([P, 2 * N], U8, name="wbw", tag="late_words", align_bytes=64)
+        nc.sync.dma_start(out=wbw[:].bitcast(I32), in_=wb_words[0].bitcast(I32))
+        subtract23(1)
+        scaled_pairs_late(1)
+        q_banks = []
         for h, cols in enumerate(halves):
-            nc.vector.tensor_tensor(out=woven(u[h]), in0=pairs(diff[:, :, cols]), in1=fk_wide, op=ALU.mult)
-        a_banks = []
-        for h in range(2):
-            codes, scales = quantise("u%d" % h, u[h], E4M3X4)
-            a_banks.append(first_stage("a%d" % h, ww, ws, codes, scales))
+            q = first_stage("q%d" % h, w2w, w2s, sxw[:, cols].bitcast(E5M2X4), sxs[:, cols])
+            nc.scalar.copy(out=qs[:, :, PAD + HALF * h : PAD + HALF * (h + 1)], in_=q[:])
+            q_banks.append(q)
+        weave(0)
+        ww = deal("ww", ww_raw)
+        uq0 = quantise("u0", u[0], E4M3X4)
+        weave(1)
+        uq1 = quantise("u1", u[1], E4M3X4)
+        a_banks = [first_stage("a%d" % h, ww, ws, *uq) for h, uq in enumerate((uq0, uq1))]
+
+        tz_picked = sb.tile([P, 2, J], F32, name="tz_picked")
+        for b in range(2):
+            nc.scalar.activation(tz_picked[:, b, :], tz_sb[:, b, :].indirect(idx2[:]), COPY)
+
+        step = sb.tile([P, PACK, J], F32, name="step")
+        for h, cols in enumerate(halves):
+            nc.vector.scalar_tensor_tensor(
+                out=step[:, :, cols],
+                in0=qs[:, :, PAD - 1 + HALF * h : PAD - 1 + HALF * (h + 1)],
+                scalar=-0.6,
+                in1=q_banks[h][:],
+                op0=ALU.mult,
+                op1=ALU.add,
+            )
 
         hid = [sb.tile([P, PACK * HALF], BF16, name="hid%d" % h, align_bytes=64) for h in range(2)]
         for h, cols in enumerate(halves):

@@ -45,11 +45,11 @@ def tile_list_two_offsetpicks_own_stepgap_timeslook_kernel(
         ws = planes[:, R : 2 * R]
         sxs = planes[:, 2 * R : 2 * R + J]
         wbs = sb.tile([P, N], U8, name="wbs", align_bytes=64)
-        w2w_raw = sb.tile([P, 2 * R], U8, name="w2w_raw", tag="late_words", align_bytes=64)
+        w2w_raw = sb.tile([P, 2 * R], U8, name="w2w_raw", align_bytes=64)
         sxw = sb.tile([P, J], U32, name="sxw", align_bytes=64)
         x01 = sb.tile([P, 2, T], F32, name="x01", tag="table")
         x23 = sb.tile([P, 2, T], F32, name="x23")
-        ow01 = sb.tile([P, 2, J], F32, name="ow01")
+        ow01 = sb.tile([P, 2, J], F32, name="ow01", tag="late_words", align_bytes=64)
         ow23 = sb.tile([P, 2, J], F32, name="ow23")
         fk_sb = sb.tile([P, PACK], F32, name="fk_sb")
 
@@ -73,13 +73,13 @@ def tile_list_two_offsetpicks_own_stepgap_timeslook_kernel(
                 in_=rows.unsqueeze(1).to_broadcast([16, P // 16, R // 4]),
             )
         nc.sync.dma_start(out=sxs[0:P:8, :].bitcast(I32), in_=sx_scales[0].bitcast(I32))
+        nc.sync.dma_start(out=w2w_raw[:].bitcast(I32), in_=w2_words[0].bitcast(I32))
         nc.sync.dma_start(out=x01[:], in_=xv[:, 0:2, :])
         nc.sync.dma_start(idx[:], offs)
-        nc.sync.dma_start(idx2[:], offs2)
         nc.sync.dma_start(out=ow01[:], in_=owv[:, 0:2, :])
         nc.sync.dma_start(out=x23[:], in_=xv[:, 2:4, :])
         nc.sync.dma_start(out=ow23[:], in_=owv[:, 2:4, :])
-        nc.sync.dma_start(out=w2w_raw[:].bitcast(I32), in_=w2_words[0].bitcast(I32))
+        nc.sync.dma_start(idx2[:], offs2)
         nc.sync.dma_start(out=sxw[:].bitcast(I32), in_=sx_words[0].rearrange("p n t -> p (n t)").bitcast(I32))
 
         nc.vector.tensor_copy(
@@ -113,6 +113,7 @@ def tile_list_two_offsetpicks_own_stepgap_timeslook_kernel(
                 )
             return bank
 
+        w2w = deal("w2w", w2w_raw)
         halves = [slice(HALF * h, HALF * (h + 1)) for h in range(2)]
         list_halves = [idx[:, 0 : HALF // 16], idx[:, HALF // 16 :]]
 
@@ -133,14 +134,17 @@ def tile_list_two_offsetpicks_own_stepgap_timeslook_kernel(
             nc.vector.tensor_tensor(out=diff01[:, :, cols], in0=picked01[:, :, cols], in1=ow01[:, :, cols], op=ALU.subtract)
         tz_sb = sb.tile([P, 2, Z], F32, name="tz_sb", tag="table")
         nc.sync.dma_start(out=tz_sb[:], in_=tz.rearrange("(h p) z -> p h z", p=P))
+        wbw = sb.tile([P, 2 * N], U8, name="wbw", tag="late_words", align_bytes=64)
+        nc.sync.dma_start(out=wbw[:].bitcast(I32), in_=wb_words[0].bitcast(I32))
         for h, cols in enumerate(halves):
             scaled_pairs(paired[h][:, 0, :], diff01[:, :, cols], fk_sb[:, 0:2])
 
         picked23 = sb.tile([P, 2, J], F32, name="picked23")
         diff23 = sb.tile([P, 2, J], F32, name="diff23")
-        for h, cols in enumerate(halves):
-            for t in range(2):
-                nc.scalar.activation(picked23[:, t, cols], x23[:, t, :].indirect(list_halves[h]), COPY)
+        for t in range(2):
+            nc.scalar.activation(picked23[:, t, halves[0]], x23[:, t, :].indirect(list_halves[0]), COPY)
+        nc.scalar.activation(picked23[:, 0, halves[1]], x23[:, 0, :].indirect(list_halves[1]), COPY)
+        nc.vector.tensor_copy(picked23[:, 1, halves[1]], x23[:, 1, :].indirect(list_halves[1]))
 
         def scaled_pairs_late(h):
             dst = paired[h][:, 1, :].rearrange("p (j t) -> p t j", t=2)
@@ -173,9 +177,6 @@ def tile_list_two_offsetpicks_own_stepgap_timeslook_kernel(
 
         subtract23(0)
         scaled_pairs_late(0)
-        w2w = deal("w2w", w2w_raw)
-        wbw = sb.tile([P, 2 * N], U8, name="wbw", tag="late_words", align_bytes=64)
-        nc.sync.dma_start(out=wbw[:].bitcast(I32), in_=wb_words[0].bitcast(I32))
         subtract23(1)
         scaled_pairs_late(1)
         q_banks = []

@@ -37,14 +37,13 @@ def tile_list_two_offsetpicks_own_stepgap_timeslook_kernel(
         idx2 = lists.tile([P, J // 16], U16, name="idx2")
 
         qs = sb.tile([P, PACK, PAD + J], F32, name="qs")
-        nc.gpsimd.memset(qs[:, :, 0:PAD], 0.0)
+        nc.gpsimd.memset(qs[:, :, PAD - 1 : PAD], 0.0)
 
         staged = shared.tile([P, 2 * R], U8, name="staged", offset=3 * R)
         planes = sb.tile([P, 2 * R + J], U8, name="planes", align_bytes=64)
         w2s = planes[:, 0:R]
         ws = planes[:, R : 2 * R]
         sxs = planes[:, 2 * R : 2 * R + J]
-        wbs = sb.tile([P, N], U8, name="wbs", align_bytes=64)
         w2w_raw = sb.tile([P, 2 * R], U8, name="w2w_raw", align_bytes=64)
         sxw = sb.tile([P, J], U32, name="sxw", align_bytes=64)
         x01 = sb.tile([P, 2, T], F32, name="x01", tag="table")
@@ -61,11 +60,6 @@ def tile_list_two_offsetpicks_own_stepgap_timeslook_kernel(
         xv = xf.rearrange("(p t) c -> p t c", t=PACK)
         owv = ow.rearrange("(p t) c -> p t c", t=PACK)
         nc.gpsimd.dma_start(out=fk_sb[:], in_=fk.rearrange("(p t) o -> p (t o)", t=PACK))
-        for quad in range(4):
-            nc.gpsimd.dma_start(
-                out=wbs[32 * quad : 32 * quad + 4, :].bitcast(I32),
-                in_=wb_scales[0, 4 * quad : 4 * quad + 4, :].bitcast(I32),
-            )
         for c, scales in enumerate((w2_scales, w_scales)):
             rows = scales[0].bitcast(I32)
             nc.sync.dma_start(
@@ -127,7 +121,7 @@ def tile_list_two_offsetpicks_own_stepgap_timeslook_kernel(
 
         paired = [sb.tile([P, 2, 2 * HALF], BF16, name="paired%d" % h) for h in range(2)]
         picked01 = shared.tile([P, 2, J], F32, name="picked01", offset=0)
-        diff01 = sb.tile([P, 2, J], F32, name="diff01")
+        diff01 = sb.tile([P, 2, J], F32, name="diff01", tag="late_scales", align_bytes=64)
         nc.scalar.activation(picked01[:, 0, :], x01[:, 0, :].indirect(idx[:]), COPY)
         nc.vector.tensor_copy(picked01[:, 1, :], x01[:, 1, :].indirect(idx[:]))
         for cols in halves:
@@ -138,6 +132,12 @@ def tile_list_two_offsetpicks_own_stepgap_timeslook_kernel(
         nc.sync.dma_start(out=wbw[:].bitcast(I32), in_=wb_words[0].bitcast(I32))
         for h, cols in enumerate(halves):
             scaled_pairs(paired[h][:, 0, :], diff01[:, :, cols], fk_sb[:, 0:2])
+        wbs = sb.tile([P, N], U8, name="wbs", tag="late_scales", align_bytes=64)
+        for quad in range(4):
+            nc.sync.dma_start(
+                out=wbs[32 * quad : 32 * quad + 4, :].bitcast(I32),
+                in_=wb_scales[0, 4 * quad : 4 * quad + 4, :].bitcast(I32),
+            )
 
         picked23 = sb.tile([P, 2, J], F32, name="picked23")
         diff23 = sb.tile([P, 2, J], F32, name="diff23")
@@ -184,27 +184,29 @@ def tile_list_two_offsetpicks_own_stepgap_timeslook_kernel(
             q = first_stage("q%d" % h, w2w, w2s, sxw[:, cols].bitcast(E5M2X4), sxs[:, cols])
             nc.scalar.copy(out=qs[:, :, PAD + HALF * h : PAD + HALF * (h + 1)], in_=q[:])
             q_banks.append(q)
-        weave(0)
-        ww = deal("ww", ww_raw)
-        uq0 = quantise("u0", u[0], E4M3X4)
-        weave(1)
-        uq1 = quantise("u1", u[1], E4M3X4)
-        a_banks = [first_stage("a%d" % h, ww, ws, *uq) for h, uq in enumerate((uq0, uq1))]
-
-        tz_picked = sb.tile([P, 2, J], F32, name="tz_picked")
-        for b in range(2):
-            nc.scalar.activation(tz_picked[:, b, :], tz_sb[:, b, :].indirect(idx2[:]), COPY)
-
         step = sb.tile([P, PACK, J], F32, name="step")
-        for h, cols in enumerate(halves):
+
+        def take_step(h):
             nc.vector.scalar_tensor_tensor(
-                out=step[:, :, cols],
+                out=step[:, :, halves[h]],
                 in0=qs[:, :, PAD - 1 + HALF * h : PAD - 1 + HALF * (h + 1)],
                 scalar=-0.6,
                 in1=q_banks[h][:],
                 op0=ALU.mult,
                 op1=ALU.add,
             )
+
+        weave(0)
+        ww = deal("ww", ww_raw)
+        a_banks = [first_stage("a0", ww, ws, *quantise("u0", u[0], E4M3X4))]
+        weave(1)
+        take_step(0)
+        a_banks.append(first_stage("a1", ww, ws, *quantise("u1", u[1], E4M3X4)))
+        take_step(1)
+
+        tz_picked = sb.tile([P, 2, J], F32, name="tz_picked")
+        for b in range(2):
+            nc.scalar.activation(tz_picked[:, b, :], tz_sb[:, b, :].indirect(idx2[:]), COPY)
 
         hid = [sb.tile([P, PACK * HALF], BF16, name="hid%d" % h, align_bytes=64) for h in range(2)]
         for h, cols in enumerate(halves):

from contextlib import ExitStack

import concourse.mybir as mybir

K, T, J, R, F, N, Z = 512, 512, 256, 512, 512, 256, 512
FLOPS = 2 * K * R * J + 2 * F * R * J + 2 * R * N * J

F32 = mybir.dt.float32
BF16 = mybir.dt.bfloat16
I32 = mybir.dt.int32
U32 = mybir.dt.uint32
U16 = mybir.dt.uint16
U8 = mybir.dt.uint8
E4M3X4 = mybir.dt.float8_e4m3fn_x4
E5M2X4 = mybir.dt.float8_e5m2_x4
E2M1X4 = mybir.dt.float4_e2m1fn_x4
ALU = mybir.AluOpType
COPY = mybir.ActivationFunctionType.Copy

P = 128
PACK = 4
HALF = 128
PAD = 4


def tile_list_two_offsetpicks_own_stepgap_timeslook_kernel(
    tc, xf, ow, fk, w_words, w_scales, sx_words, sx_scales, w2_words, w2_scales, wb_words, wb_scales, tz, offs, offs2, out
):
    nc = tc.nc
    with ExitStack() as ctx:
        lists = ctx.enter_context(tc.tile_pool(name="lists", bufs=1))
        sb = ctx.enter_context(tc.tile_pool(name="sb", bufs=1))
        shared = ctx.enter_context(tc.tile_pool(name="shared", bufs=1))
        ps = ctx.enter_context(tc.psum_pool(name="ps", bufs=1))

        idx = lists.tile([P, J // 16], U16, name="idx")
        idx2 = lists.tile([P, J // 16], U16, name="idx2")

        qs = sb.tile([P, PACK, PAD + J], F32, name="qs")
        nc.gpsimd.memset(qs[:, :, PAD - 1 : PAD], 0.0)

        staged = shared.tile([P, 2 * R], U8, name="staged", offset=3 * R)
        planes = sb.tile([P, 2 * R + J], U8, name="planes", align_bytes=64)
        w2s = planes[:, 0:R]
        ws = planes[:, R : 2 * R]
        sxs = planes[:, 2 * R : 2 * R + J]
        w2w_raw = sb.tile([P, 2 * R], U8, name="w2w_raw", align_bytes=64)
        sxw = sb.tile([P, J], U32, name="sxw", align_bytes=64)
        x01 = sb.tile([P, 2, T], F32, name="x01", tag="table")
        x23 = sb.tile([P, 2, T], F32, name="x23")
        ow01 = sb.tile([P, 2, J], F32, name="ow01", tag="late_words", align_bytes=64)
        ow23 = sb.tile([P, 2, J], F32, name="ow23")
        fk_sb = sb.tile([P, PACK], F32, name="fk_sb")

        warm_in = sb.tile([P, 8], F32, name="warm_in")
        warm_out = sb.tile([P, 8], F32, name="warm_out")
        nc.gpsimd.memset(warm_in[:], 0.0)
        nc.scalar.activation(warm_out[:], warm_in[:], COPY)

        xv = xf.rearrange("(p t) c -> p t c", t=PACK)
        owv = ow.rearrange("(p t) c -> p t c", t=PACK)
        nc.gpsimd.dma_start(out=fk_sb[:], in_=fk.rearrange("(p t) o -> p (t o)", t=PACK))
        for c, scales in enumerate((w2_scales, w_scales)):
            rows = scales[0].bitcast(I32)
            nc.sync.dma_start(
                out=staged[:, R * c : R * (c + 1)].bitcast(I32),
                in_=rows.unsqueeze(1).to_broadcast([16, P // 16, R // 4]),
            )
        nc.sync.dma_start(out=sxs[0:P:8, :].bitcast(I32), in_=sx_scales[0].bitcast(I32))
        nc.sync.dma_start(out=w2w_raw[:].bitcast(I32), in_=w2_words[0].bitcast(I32))
        nc.sync.dma_start(out=x01[:], in_=xv[:, 0:2, :])
        nc.sync.dma_start(idx[:], offs)
        nc.sync.dma_start(out=ow01[:], in_=owv[:, 0:2, :])
        nc.sync.dma_start(out=x23[:], in_=xv[:, 2:4, :])
        nc.sync.dma_start(out=ow23[:], in_=owv[:, 2:4, :])
        nc.sync.dma_start(idx2[:], offs2)
        nc.sync.dma_start(out=sxw[:].bitcast(I32), in_=sx_words[0].rearrange("p n t -> p (n t)").bitcast(I32))

        nc.vector.tensor_copy(
            out=planes[:, 0 : 2 * R].rearrange("p (w t c i) -> p w c t i", w=2, t=PACK, i=16),
            in_=staged[:].rearrange("p (w c i t) -> p w c t i", w=2, t=PACK, i=16),
        )
        for r in range(1, 4):
            nc.sync.dma_start(out=planes[r:P:32, :].bitcast(I32), in_=planes[8 * r : P : 32, :].bitcast(I32))
        ww_raw = shared.tile([P, 2 * R], U8, name="ww_raw", offset=4 * R)
        nc.sync.dma_start(out=ww_raw[:].bitcast(I32), in_=w_words[0].bitcast(I32))

        def deal(name, raw):
            t = sb.tile([P, 2 * R], U8, name=name, align_bytes=64)
            nc.vector.tensor_copy(
                out=t[:].bitcast(U16).rearrange("p (t c i) -> p c t i", t=PACK, i=8),
                in_=raw[:].bitcast(U16).rearrange("p (c i t) -> p c t i", t=PACK, i=8),
            )
            return t

        def first_stage(name, words, scales, rhs, rhs_scale):
            bank = ps.tile([P, PACK, HALF], F32, name=name)
            for t in range(PACK):
                nc.tensor.matmul_mx(
                    out=bank[:, t, :],
                    lhsT=words[:, 2 * P * t : 2 * P * (t + 1)].bitcast(E2M1X4),
                    lhsT_scale=scales[:, P * t : P * (t + 1)],
                    rhs=rhs,
                    rhs_scale=rhs_scale,
                    start=True,
                    stop=True,
                )
            return bank

        w2w = deal("w2w", w2w_raw)
        halves = [slice(HALF * h, HALF * (h + 1)) for h in range(2)]
        list_halves = [idx[:, 0 : HALF // 16], idx[:, HALF // 16 :]]

        def scaled_pairs(dst, diff, factors):
            nc.vector.tensor_tensor(
                out=dst.rearrange("p (c i t) -> p c t i", t=2, i=4),
                in0=diff.rearrange("p t (c i) -> p c t i", i=4),
                in1=factors.unsqueeze(1).unsqueeze(3).to_broadcast([P, HALF // 4, 2, 4]),
                op=ALU.mult,
            )

        paired = [sb.tile([P, 2, 2 * HALF], BF16, name="paired%d" % h) for h in range(2)]
        picked01 = shared.tile([P, 2, J], F32, name="picked01", offset=0)
        diff01 = sb.tile([P, 2, J], F32, name="diff01", tag="late_scales", align_bytes=64)
        nc.scalar.activation(picked01[:, 0, :], x01[:, 0, :].indirect(idx[:]), COPY)
        nc.vector.tensor_copy(picked01[:, 1, :], x01[:, 1, :].indirect(idx[:]))
        for cols in halves:
            nc.vector.tensor_tensor(out=diff01[:, :, cols], in0=picked01[:, :, cols], in1=ow01[:, :, cols], op=ALU.subtract)
        tz_sb = sb.tile([P, 2, Z], F32, name="tz_sb", tag="table")
        nc.sync.dma_start(out=tz_sb[:], in_=tz.rearrange("(h p) z -> p h z", p=P))
        wbw = sb.tile([P, 2 * N], U8, name="wbw", tag="late_words", align_bytes=64)
        nc.sync.dma_start(out=wbw[:].bitcast(I32), in_=wb_words[0].bitcast(I32))
        for h, cols in enumerate(halves):
            scaled_pairs(paired[h][:, 0, :], diff01[:, :, cols], fk_sb[:, 0:2])
        wbs = sb.tile([P, N], U8, name="wbs", tag="late_scales", align_bytes=64)
        for quad in range(4):
            nc.sync.dma_start(
                out=wbs[32 * quad : 32 * quad + 4, :].bitcast(I32),
                in_=wb_scales[0, 4 * quad : 4 * quad + 4, :].bitcast(I32),
            )

        picked23 = sb.tile([P, 2, J], F32, name="picked23")
        diff23 = sb.tile([P, 2, J], F32, name="diff23")
        for t in range(2):
            nc.scalar.activation(picked23[:, t, halves[0]], x23[:, t, :].indirect(list_halves[0]), COPY)
        nc.scalar.activation(picked23[:, 0, halves[1]], x23[:, 0, :].indirect(list_halves[1]), COPY)
        nc.vector.tensor_copy(picked23[:, 1, halves[1]], x23[:, 1, :].indirect(list_halves[1]))

        def scaled_pairs_late(h):
            dst = paired[h][:, 1, :].rearrange("p (j t) -> p t j", t=2)
            for t in range(2):
                nc.scalar.activation(dst[:, t, :], diff23[:, t, halves[h]], COPY, scale=fk_sb[:, 2 + t : 3 + t])

        def pairs(ap):
            return ap.rearrange("p t (c i) -> p c t i", i=2)

        def woven(t):
            return t[:].rearrange("p (c i t) -> p c t i", t=PACK, i=2)

        def quantise(name, src, dtype):
            codes = sb.tile([P, HALF], U32, name=name + "_codes", align_bytes=64)
            scales = sb.tile([P, HALF], U8, name=name + "_scales", align_bytes=64)
            nc.vector.quantize_mx(out=codes[:].bitcast(dtype), scales=scales[:], in_=src[:])
            return codes[:].bitcast(dtype), scales[:]

        def subtract23(h):
            cols = halves[h]
            nc.vector.tensor_tensor(out=diff23[:, :, cols], in0=picked23[:, :, cols], in1=ow23[:, :, cols], op=ALU.subtract)

        u = [sb.tile([P, PACK * HALF], BF16, name="u%d" % h, align_bytes=64) for h in range(2)]

        def weave(h):
            nc.vector.tensor_copy(
                out=u[h][:].bitcast(I32).rearrange("p (c i u) -> p c u i", u=2, i=2),
                in_=paired[h][:].bitcast(I32).rearrange("p u (c i) -> p c u i", i=2),
            )

        subtract23(0)
        scaled_pairs_late(0)
        subtract23(1)
        scaled_pairs_late(1)
        q_banks = []
        for h, cols in enumerate(halves):
            q = first_stage("q%d" % h, w2w, w2s, sxw[:, cols].bitcast(E5M2X4), sxs[:, cols])
            nc.scalar.copy(out=qs[:, :, PAD + HALF * h : PAD + HALF * (h + 1)], in_=q[:])
            q_banks.append(q)
        step = sb.tile([P, PACK, J], F32, name="step")

        def take_step(h):
            nc.vector.scalar_tensor_tensor(
                out=step[:, :, halves[h]],
                in0=qs[:, :, PAD - 1 + HALF * h : PAD - 1 + HALF * (h + 1)],
                scalar=-0.6,
                in1=q_banks[h][:],
                op0=ALU.mult,
                op1=ALU.add,
            )

        weave(0)
        ww = deal("ww", ww_raw)
        a_banks = [first_stage("a0", ww, ws, *quantise("u0", u[0], E4M3X4))]
        weave(1)
        take_step(0)
        a_banks.append(first_stage("a1", ww, ws, *quantise("u1", u[1], E4M3X4)))
        take_step(1)

        tz_picked = sb.tile([P, 2, J], F32, name="tz_picked")
        for b in range(2):
            nc.scalar.activation(tz_picked[:, b, :], tz_sb[:, b, :].indirect(idx2[:]), COPY)

        hid = [sb.tile([P, PACK * HALF], BF16, name="hid%d" % h, align_bytes=64) for h in range(2)]
        for h, cols in enumerate(halves):
            nc.vector.tensor_tensor(out=woven(hid[h]), in0=pairs(a_banks[h][:]), in1=pairs(step[:, :, cols]), op=ALU.max)
        p_banks = []
        for h in range(2):
            codes, scales = quantise("hid%d" % h, hid[h], E5M2X4)
            bank = ps.tile([P, 2, HALF], F32, name="p%d" % h)
            for b in range(2):
                nc.tensor.matmul_mx(
                    out=bank[:, b, :],
                    lhsT=wbw[:, 2 * P * b : 2 * P * (b + 1)].bitcast(E2M1X4),
                    lhsT_scale=wbs[:, P * b : P * (b + 1)],
                    rhs=codes,
                    rhs_scale=scales,
                    start=True,
                    stop=True,
                )
            p_banks.append(bank)

        ov = out.rearrange("(b p) j -> p b j", p=P)
        for h, cols in enumerate(halves):
            y = sb.tile([P, 2, HALF], F32, name="y%d" % h)
            nc.vector.tensor_tensor(out=y[:], in0=p_banks[h][:], in1=tz_picked[:, :, cols], op=ALU.mult)
            queue = nc.sync if h == 0 else nc.scalar
            queue.dma_start(out=ov[:, :, cols], in_=y[:])
